import numpy as np
import ml_dtypes


def mxq(x, axis, fmt="e4m3"):
    dtype, down = {"e4m3": (ml_dtypes.float8_e4m3fn, 7), "e5m2": (ml_dtypes.float8_e5m2, 14)}[fmt]
    v = np.moveaxis(np.asarray(x, np.float32).astype(ml_dtypes.bfloat16).astype(np.float64), axis, -1)
    blocks = v.reshape(v.shape[:-1] + (-1, 32))
    amax = np.abs(blocks).max(-1, keepdims=True)
    byte = np.maximum(np.where(amax > 0, np.frexp(amax)[1] - 1 + 127, 0) - down, 1)
    scale = np.exp2(byte - 127.0)
    codes = (blocks / scale).astype(np.float32).astype(dtype).astype(np.float64)
    return np.moveaxis((codes * scale).reshape(v.shape), -1, axis)


WIDE = False


def mx_kscale(k):
    if not WIDE:
        return np.ones(k)
    levels = np.array([10, -10, 5, -5, 0])
    if k % 512:
        return np.exp2(np.random.permutation(np.resize(levels, k // 32))).repeat(32)
    a = np.empty((k // 512, 16))
    for p in range(k // 512):
        a[p, :8] = np.random.permutation(np.resize(levels, 8))
        for g in range(8):
            far = levels[np.abs(levels - a[p, g]) >= 10]
            a[p, g + 8] = far[np.random.randint(len(far))]
    return np.exp2(a.ravel()).repeat(32)


def f64(x):
    return np.asarray(x).astype(np.float64)


def striped(idx):
    return np.tile(np.asarray(idx).reshape(-1, 16).T, (8, 1)).astype(np.uint16)


def unstriped(offs):
    return offs[:16].T.reshape(-1).astype(np.int64)


def striped8(idx):
    return np.asarray(idx).reshape(8, -1, 16).transpose(0, 2, 1).reshape(128, -1).astype(np.uint16)


def unstriped8(offs):
    return offs.reshape(8, 16, -1).transpose(0, 2, 1).reshape(8, -1).astype(np.int64)


def pick8(x, idx, run):
    r = np.arange(len(x))
    return x[r[:, None], idx[r % (8 * run) // run]]


E2M1 = np.array([0.0, 0.5, 1.0, 1.5, 2.0, 3.0, 4.0, 6.0, -0.0, -0.5, -1.0, -1.5, -2.0, -3.0, -4.0, -6.0])


def pack_weight(w, fmt):
    k, n = w.shape
    w = f64(np.asarray(w, np.float32).astype(ml_dtypes.bfloat16)).reshape(k // 32, 32, n)
    amax = np.abs(w).max(1)
    if fmt == "e4m3":
        byte = np.frexp(amax)[1] - 1 + 127 - 7
    else:
        mant, ex = np.frexp(amax / 6.0)
        byte = np.where(mant > 0.5, ex, ex - 1) + 127
    byte = np.clip(np.where(amax > 0, byte, 1), 1, 254)
    scaled = (w * np.exp2(127.0 - byte)[:, None, :]).reshape(k, n).astype(np.float32)
    by_word = np.ascontiguousarray(scaled.reshape(k // 512, 128, 4, n).transpose(0, 1, 3, 2))
    if fmt == "e4m3":
        words = by_word.astype(ml_dtypes.float8_e4m3fn).view(np.uint8)
    else:
        c = by_word.astype(ml_dtypes.float4_e2m1fn).view(np.uint8) & 0xF
        words = (c[..., 0::2] | (c[..., 1::2] << 4)).reshape(k // 512, 128, 2 * n)
    return np.ascontiguousarray(words), np.ascontiguousarray(byte.astype(np.uint8).reshape(k // 512, 16, n))


def unpack_weight(words, scales, fmt):
    g, _, n = scales.shape
    words = np.ascontiguousarray(words).reshape(g, 128, n, -1)
    if fmt == "e4m3":
        vals = words.view(ml_dtypes.float8_e4m3fn).astype(np.float64)
    else:
        nib = np.empty((g, 128, n, 4), np.uint8)
        nib[..., 0::2] = words & 0xF
        nib[..., 1::2] = words >> 4
        vals = E2M1[nib]
    vals = vals * np.repeat(np.exp2(scales.astype(np.float64) - 127.0), 8, axis=1)[..., None]
    return vals.transpose(0, 1, 3, 2).reshape(g * 512, n)


K, J, R, T, C, O, U, D, N, S = 512, 512, 512, 1024, 1024, 256, 256, 512, 256, 1024


def setup_inputs():
    n = np.random.standard_normal
    idx = np.random.permutation(T)[:J]
    idx2 = np.stack([np.random.permutation(C)[:J] for _ in range(8)])
    idx3 = np.stack([np.random.permutation(C)[:J] for _ in range(8)])
    idx4 = np.stack([np.random.permutation(C)[:O] for _ in range(8)])
    idx5 = np.stack([np.random.permutation(C)[:U] for _ in range(8)])
    idx6 = np.random.permutation(S)[:N]
    fk = mx_kscale(K)
    fr = mx_kscale(R)
    xtp = pack_weight(n((K, T)) * fk[:, None], "e2m1")
    wp = pack_weight(n((K, R)) * 1 / np.sqrt(K) / fk[:, None] * fr, "e4m3")
    w2p = pack_weight(n((K, R)) * 1 / np.sqrt(K) / fk[:, None] * fr, "e4m3")
    vsp = pack_weight(n((R, S)) * 1 / np.sqrt(R) / fr[:, None], "e4m3")
    return {
        "xt_words": xtp[0],
        "xt_scales": xtp[1],
        "w_words": wp[0],
        "w_scales": wp[1],
        "w2_words": w2p[0],
        "w2_scales": w2p[1],
        "sa": (np.random.uniform(0.5, 1.6, (R, 1))).astype(np.float32),
        "sb": (np.random.uniform(0.5, 1.6, (R, 1))).astype(np.float32),
        "vs_words": vsp[0],
        "vs_scales": vsp[1],
        "offs": striped(idx),
        "offs2": striped8(idx2),
        "offs3": striped8(idx3),
        "offs4": striped8(idx4),
        "offs5": striped8(idx5),
        "offs6": striped(idx6),
    }


def reference(xt_words, xt_scales, w_words, w_scales, w2_words, w2_scales, sa, sb, vs_words, vs_scales, offs, offs2, offs3, offs4, offs5, offs6):
    idx = unstriped(offs)
    idx2 = unstriped8(offs2)
    idx3 = unstriped8(offs3)
    idx4 = unstriped8(offs4)
    idx5 = unstriped8(offs5)
    idx6 = unstriped(offs6)
    xtu = unpack_weight(xt_words, xt_scales, "e2m1")
    wu = unpack_weight(w_words, w_scales, "e4m3")
    w2u = unpack_weight(w2_words, w2_scales, "e4m3")
    vsu = unpack_weight(vs_words, vs_scales, "e4m3")
    xtidxg = xtu[:, idx]
    a = wu.T @ xtidxg
    b = w2u.T @ xtidxg
    pw = np.zeros((R, C))
    pw[np.arange(R)[:, None], idx2[np.arange(R) % 512 // 64]] = a
    pv = np.zeros((R, C))
    pv[np.arange(R)[:, None], idx3[np.arange(R) % 512 // 64]] = b
    ph = np.maximum(pw, pv)
    pl = np.minimum(pw, pv)
    h1 = pick8(ph, idx4, 64) * f64(sa)
    h2 = pick8(pl, idx5, 64) * f64(sb)
    hid = np.concatenate([h1, h2], axis=1)
    vsidx6g = vsu[:, idx6]
    hidq = mxq(hid, 0, "e4m3")
    y = vsidx6g.T @ hidq
    return y

@@ -1,0 +1,271 @@
+from contextlib import ExitStack
+
+import concourse.mybir as mybir
+
+K, J, R, T, C, O, U, D, N, S = 512, 512, 512, 1024, 1024, 256, 256, 512, 256, 1024
+FLOPS = 2 * (2 * K * R * J + R * N * D)
+
+F32 = mybir.dt.float32
+BF16 = mybir.dt.bfloat16
+I32 = mybir.dt.int32
+U32 = mybir.dt.uint32
+U16 = mybir.dt.uint16
+U8 = mybir.dt.uint8
+FP8X4 = mybir.dt.float8_e4m3fn_x4
+FP4X4 = mybir.dt.float4_e2m1fn_x4
+COPY = mybir.ActivationFunctionType.Copy
+ALU = mybir.AluOpType
+
+P = 128
+PACK = 4
+QUAD = 32
+
+
+def tile_picked_tokens_plain_twin_winnersides_store_plain_kernel(
+    tc, xt_words, xt_scales, w_words, w_scales, w2_words, w2_scales, sa, sb, vs_words, vs_scales,
+    offs, offs2, offs3, offs4, offs5, offs6, out
+):
+    nc = tc.nc
+    with ExitStack() as ctx:
+        lists = ctx.enter_context(tc.tile_pool(name="lists", bufs=1))
+        pool = ctx.enter_context(tc.tile_pool(name="pool", bufs=1))
+        psum = ctx.enter_context(tc.psum_pool(name="psum", bufs=1))
+
+        def sb_tile(shape, dtype, name, tag=None):
+            return pool.tile(shape, dtype, name=name, tag=tag or name, align_bytes=64)
+
+        def list_tile(src, name):
+            return lists.tile([P, src.shape[1]], U16, name=name)
+
+        l_tok = list_tile(offs, "l_tok")
+        l_pw = list_tile(offs2, "l_pw")
+        l_pv = list_tile(offs3, "l_pv")
+        l_win = list_tile(offs4, "l_win")
+        l_los = list_tile(offs5, "l_los")
+        l_vs = list_tile(offs6, "l_vs")
+
+        def cols16(a, b):
+            return slice(a // 16, b // 16)
+
+        x_stage = sb_tile([P, 2 * T // 4], I32, "x_stage", "slot_xstage")
+        w_stage = sb_tile([P, 4 * R // 4], I32, "w_stage", "slot_wstage")
+        x_win = sb_tile([P, 2 * T], U8, "x_win", "slot_xwin")
+        w_raw = sb_tile([P, R], I32, "w_raw", "slot_wraw")
+        xs_src = xt_scales[0].bitcast(I32).rearrange("(h q i) c -> h i q c", h=2, q=2)
+        nc.sync.dma_start(l_tok[:], offs)
+        for h, queue in enumerate((nc.sync, nc.scalar)):
+            queue.dma_start(
+                x_stage[64 * h : 64 * h + 4, :].rearrange("i (q c) -> i q c", q=2), xs_src[h]
+            )
+        nc.scalar.dma_start(
+            w_stage[0:4, :].rearrange("i (q c) -> i q c", q=4),
+            w_scales[0].bitcast(I32).rearrange("(q i) c -> i q c", q=4),
+        )
+        nc.sync.dma_start(x_win[:].bitcast(I32), xt_words[0].bitcast(I32))
+        nc.scalar.dma_start(w_raw[:], w_words[0].rearrange("p n t -> p (n t)").bitcast(I32))
+        nc.sync.dma_start(l_pw[:], offs2)
+
+        xs_win = sb_tile([P, T], U8, "xs_win", "slot_xswin")
+        ws_plane = sb_tile([P, R], U8, "ws_plane", "slot_wsplane")
+        w2s_plane = sb_tile([P, R], U8, "w2s_plane", "slot_w2splane")
+        vss_win = sb_tile([P, S], U8, "vss_win")
+        for plane in (xs_win, ws_plane, w2s_plane, vss_win):
+            nc.vector.memset(plane[:].bitcast(I32), 0)
+
+        pw = [None] * PACK
+        pv = [None] * PACK
+        for t in (0, 1, 2):
+            pw[t] = sb_tile([P, C], F32, "pw%d" % t)
+            nc.vector.memset(pw[t][:].bitcast(I32), 0)
+
+        nc.sync.dma_start(l_pv[:], offs3)
+        w2_raw = sb_tile([P, R], I32, "w2_raw", "slot_w2raw")
+        nc.sync.dma_start(w2_raw[:], w2_words[0].rearrange("p n t -> p (n t)").bitcast(I32))
+        for q in range(4):
+            nc.sync.dma_start(
+                w2s_plane[QUAD * q : QUAD * q + 4, :].bitcast(I32),
+                w2_scales[0, 4 * q : 4 * q + 4, :].bitcast(I32),
+            )
+        nc.sync.dma_start(l_vs[:], offs6)
+        vs_win = sb_tile([P, S], I32, "vs_win")
+        nc.sync.dma_start(vs_win[:], vs_words[0].rearrange("p n t -> p (n t)").bitcast(I32))
+        for q in range(4):
+            nc.sync.dma_start(
+                vss_win[QUAD * q : QUAD * q + 4, :].bitcast(I32),
+                vs_scales[0, 4 * q : 4 * q + 4, :].bitcast(I32),
+            )
+        nc.sync.dma_start(l_win[:], offs4)
+        nc.sync.dma_start(l_los[:], offs5)
+        sa_t = sb_tile([P, PACK], F32, "sa_t")
+        sb_t = sb_tile([P, PACK], F32, "sb_t")
+        nc.sync.dma_start(sa_t[:], sa.rearrange("(p t) o -> p (t o)", t=PACK))
+        nc.sync.dma_start(sb_t[:], sb.rearrange("(p t) o -> p (t o)", t=PACK))
+
+        ws_i = ws_plane[:].bitcast(I32)
+        for q in range(4):
+            nc.vector.tensor_copy(
+                ws_i[QUAD * q : QUAD * q + 4, :], w_stage[0:4, q * (R // 4) : (q + 1) * (R // 4)]
+            )
+
+        xs_i = xs_win[:].bitcast(I32)
+        for q in range(4):
+            h, k = divmod(q, 2)
+            nc.vector.tensor_copy(
+                xs_i[QUAD * q : QUAD * q + 4, :],
+                x_stage[64 * h : 64 * h + 4, k * (T // 4) : (k + 1) * (T // 4)],
+            )
+        xg = sb_tile([P, 2 * J], U8, "xg")
+        xsg = sb_tile([P, J], U8, "xsg")
+
+        def gather_x(a, b):
+            nc.vector.tensor_copy(
+                xg[:].bitcast(U16)[:, a:b], x_win[:].bitcast(U16).indirect(l_tok[:, cols16(a, b)])
+            )
+            nc.vector.tensor_copy(xsg[:, a:b], xs_win[:].indirect(l_tok[:, cols16(a, b)]))
+
+        wd = sb_tile([P, R], I32, "wd")
+        wsd = sb_tile([P, R], U8, "wsd")
+
+        def deal(words, plane, raw_words, raw_plane, t0, t1):
+            cols = slice(t0 * P, t1 * P)
+            nc.vector.tensor_copy(
+                words[:, cols].rearrange("p (t m) -> p t m", m=P),
+                raw_words[:].rearrange("p (m t) -> p t m", t=PACK)[:, t0:t1, :],
+            )
+            nc.vector.tensor_copy(
+                plane[:, cols].rearrange("p (t m) -> p t m", m=P),
+                raw_plane[:].rearrange("p (m t) -> p t m", t=PACK)[:, t0:t1, :],
+            )
+
+        def product(bank, words, plane, t, a, b):
+            nc.tensor.matmul_mx(
+                out=bank[:, a:b],
+                lhsT=words[:, t * P : (t + 1) * P].bitcast(FP8X4),
+                lhsT_scale=plane[:, t * P : (t + 1) * P],
+                rhs=xg[:, 2 * a : 2 * b].bitcast(FP4X4),
+                rhs_scale=xsg[:, a:b],
+                start=True,
+                stop=True,
+            )
+
+        a_ps = [psum.tile([P, J], F32, name="a_ps%d" % t, tag="bank_a%d" % t) for t in range(PACK)]
+        a_sb = [sb_tile([P, J], F32, "a_sb%d" % t) for t in range(PACK)]
+
+        def scatter(board, vals, lst, a, b):
+            nc.scalar.activation(board[:].indirect(lst[:, cols16(a, b)]), vals[:, a:b], COPY)
+
+        def a_piece(t, cuts, on_scalar=False):
+            for a, b in zip(cuts, cuts[1:]):
+                product(a_ps[t], wd, wsd, t, a, b)
+            a, b = cuts[0], cuts[-1]
+            if on_scalar:
+                nc.scalar.activation(a_sb[t][:, a:b], a_ps[t][:, a:b], COPY)
+            else:
+                nc.vector.tensor_copy(a_sb[t][:, a:b], a_ps[t][:, a:b])
+            scatter(pw[t], a_sb[t], l_pw, a, b)
+
+        deal(wd, wsd, w_raw, ws_plane, 0, 1)
+        gather_x(0, 128)
+        a_piece(0, (0, 128), True)
+        deal(wd, wsd, w_raw, ws_plane, 1, 2)
+        a_piece(1, (0, 128))
+        gather_x(128, 256)
+        a_piece(0, (128, 256))
+        a_piece(1, (128, 256))
+        gather_x(256, 512)
+        a_piece(0, (256, 512))
+        a_piece(1, (256, 512))
+        deal(wd, wsd, w_raw, ws_plane, 2, 4)
+        a_piece(2, (0, 512))
+        pw[3] = sb_tile([P, C], F32, "pw3", "slot_xwin")
+        nc.vector.memset(pw[3][:].bitcast(I32), 0)
+        a_piece(3, (0, 512))
+
+        w2d = sb_tile([P, R], I32, "w2d")
+        w2sd = sb_tile([P, R], U8, "w2sd")
+        deal(w2d, w2sd, w2_raw, w2s_plane, 0, 4)
+        b_ps = [psum.tile([P, J], F32, name="b_ps%d" % t, tag="bank_b%d" % t) for t in range(PACK)]
+        b_sb = [sb_tile([P, J], F32, "b_sb%d" % t, "slot_b%d" % t) for t in range(PACK)]
+        pv_tags = ("slot_wraw", "slot_wsplane", "slot_w2raw", "slot_w2splane")
+        for t in range(PACK):
+            product(b_ps[t], w2d, w2sd, t, 0, J)
+            nc.vector.tensor_copy(b_sb[t][:], b_ps[t][:])
+            pv[t] = sb_tile([P, C], F32, "pv%d" % t, pv_tags[t])
+            nc.vector.memset(pv[t][:].bitcast(I32), 0)
+
+        vg = sb_tile([P, N], U32, "vg")
+        vsg = sb_tile([P, N], U8, "vsg")
+        nc.vector.tensor_copy(vg[:], vs_win[:].bitcast(U32).indirect(l_vs[:]))
+        nc.vector.tensor_copy(vsg[:], vss_win[:].indirect(l_vs[:]))
+
+        ph = [None] * PACK
+        pl = [None] * PACK
+        for t in range(PACK):
+            scatter(pv[t], b_sb[t], l_pv, 0, J)
+            ph[t] = sb_tile([P, C], F32, "ph%d" % t, "slot_ph%d" % t)
+            pl[t] = sb_tile([P, C], F32, "pl%d" % t, "slot_pl%d" % t)
+            nc.vector.tensor_tensor(ph[t][:], pw[t][:], pv[t][:], ALU.max)
+            nc.vector.tensor_tensor(pl[t][:], pw[t][:], pv[t][:], ALU.min)
+
+        def fetch(side, boards, lst, gain, tag):
+            planes = sb_tile([P, PACK, O], BF16, "planes%d" % side, tag)
+            for t in range(PACK):
+                nc.scalar.activation(
+                    planes[:, t, :], boards[t][:].indirect(lst[:]), COPY, scale=gain[:, t : t + 1]
+                )
+            return planes
+
+        def weave(planes, a, b, name):
+            woven = sb_tile([P, b - a, PACK], BF16, "woven" + name)
+            nc.vector.tensor_copy(
+                woven[:].rearrange("p (c i) t -> p c t i", i=4),
+                planes[:, :, a:b].rearrange("p t (c i) -> p c t i", i=4),
+            )
+            return woven
+
+        def quantise(woven, name):
+            width = woven.shape[1]
+            hq = sb_tile([P, width], U32, "hq" + name)
+            hs = sb_tile([P, width], U8, "hs" + name)
+            nc.vector.quantize_mx(
+                out=hq[:].bitcast(FP8X4), scales=hs[:], in_=woven[:].rearrange("p c t -> p (c t)")
+            )
+            return hq, hs
+
+        def last_product(hq, hs, half, bank):
+            rows = slice(half * P, (half + 1) * P)
+            y_ps = psum.tile([P, hq.shape[1]], F32, name="y_" + bank, tag=bank)
+            nc.tensor.matmul_mx(
+                out=y_ps[:],
+                lhsT=vg[:, rows].bitcast(FP8X4),
+                lhsT_scale=vsg[:, rows],
+                rhs=hq[:].bitcast(FP8X4),
+                rhs_scale=hs[:],
+                start=True,
+                stop=True,
+            )
+            return y_ps
+
+        win_planes = fetch(0, ph, l_win, sa_t, "slot_b3")
+        win_q = quantise(weave(win_planes, 0, O, "w"), "w")
+        win_ps = [last_product(*win_q, half, "bank_a%d" % half) for half in range(2)]
+        los_planes = fetch(1, pl, l_los, sb_t, "slot_ph3")
+        y_win = sb_tile([P, 2, O], F32, "y_win", "slot_pl3")
+        for half in range(2):
+            nc.scalar.copy(y_win[:, half, :], win_ps[half][:])
+        nc.sync.dma_start(out.rearrange("(h p) d -> p h d", h=2)[:, :, 0:O], y_win[:])
+        HALF = U // 2
+        los_w = [weave(los_planes, j * HALF, (j + 1) * HALF, "l%d" % j) for j in range(2)]
+        los_q = [quantise(los_w[j], "l%d" % j) for j in range(2)]
+        for j in range(2):
+            cols = slice(O + j * HALF, O + (j + 1) * HALF)
+            for half in range(2):
+                rows = slice(half * P, (half + 1) * P)
+                y_ps = last_product(*los_q[j], half, "bank_b%d" % (2 * j + half))
+                y_sb = sb_tile([P, HALF], F32, "y_los%d%d" % (j, half))
+                if half == 0:
+                    nc.scalar.copy(y_sb[:], y_ps[:])
+                    nc.scalar.dma_start(out[rows, cols], y_sb[:])
+                else:
+                    nc.vector.tensor_copy(y_sb[:], y_ps[:])
+                    nc.sync.dma_start(out[rows, cols], y_sb[:])

@@ -29,10 +29,14 @@ def tile_picked_tokens_plain_twin_winnersides_store_plain_kernel(
     with ExitStack() as ctx:
         lists = ctx.enter_context(tc.tile_pool(name="lists", bufs=1))
         pool = ctx.enter_context(tc.tile_pool(name="pool", bufs=1))
+        reuse = ctx.enter_context(tc.tile_pool(name="reuse", bufs=1))
         psum = ctx.enter_context(tc.psum_pool(name="psum", bufs=1))
 
         def sb_tile(shape, dtype, name, tag=None):
             return pool.tile(shape, dtype, name=name, tag=tag or name, align_bytes=64)
+
+        def placed(shape, dtype, name, offset):
+            return reuse.tile(shape, dtype, name=name, offset=offset, align_bytes=64)
 
         def list_tile(src, name):
             return lists.tile([P, src.shape[1]], U16, name=name)
@@ -47,53 +51,71 @@ def tile_picked_tokens_plain_twin_winnersides_store_plain_kernel(
         def cols16(a, b):
             return slice(a // 16, b // 16)
 
-        x_stage = sb_tile([P, 2 * T // 4], I32, "x_stage", "slot_xstage")
-        w_stage = sb_tile([P, 4 * R // 4], I32, "w_stage", "slot_wstage")
-        x_win = sb_tile([P, 2 * T], U8, "x_win", "slot_xwin")
-        w_raw = sb_tile([P, R], I32, "w_raw", "slot_wraw")
-        xs_src = xt_scales[0].bitcast(I32).rearrange("(h q i) c -> h i q c", h=2, q=2)
+        x_stage = sb_tile([P, 2 * T // 4], I32, "x_stage")
+        w_stage = sb_tile([P, 2 * R // 4], I32, "w_stage")
+        x_win = sb_tile([P, 2 * T], U8, "x_win")
+        w_raw = placed([P, R], I32, "w_raw", 0)
+
+        def stage_rows(queue, stage, src, h):
+            rows = src[0].bitcast(I32).rearrange("(h q i) c -> h i q c", h=2, q=2)
+            queue.dma_start(stage[64 * h : 64 * h + 4, :].rearrange("i (q c) -> i q c", q=2), rows[h])
+
+        def spread_rows(plane, stage, share=False):
+            words = plane[:].bitcast(I32)
+            width = words.shape[1]
+            for q in range(4):
+                h, k = divmod(q, 2)
+                dst = words[QUAD * q : QUAD * q + 4, :]
+                src = stage[64 * h : 64 * h + 4, k * width : (k + 1) * width]
+                if share and k == 0:
+                    nc.scalar.copy(dst.bitcast(U32), src.bitcast(U32))
+                else:
+                    nc.vector.tensor_copy(dst, src)
+
+        def load_scale_rows(plane, src):
+            for q in range(4):
+                nc.sync.dma_start(
+                    plane[QUAD * q : QUAD * q + 4, :].bitcast(I32), src[0, 4 * q : 4 * q + 4, :].bitcast(I32)
+                )
+
+        def load_words(queue, dst, src):
+            queue.dma_start(dst[:], src[0].rearrange("p n t -> p (n t)").bitcast(I32))
+
         nc.sync.dma_start(l_tok[:], offs)
         for h, queue in enumerate((nc.sync, nc.scalar)):
-            queue.dma_start(
-                x_stage[64 * h : 64 * h + 4, :].rearrange("i (q c) -> i q c", q=2), xs_src[h]
-            )
-        nc.scalar.dma_start(
-            w_stage[0:4, :].rearrange("i (q c) -> i q c", q=4),
-            w_scales[0].bitcast(I32).rearrange("(q i) c -> i q c", q=4),
-        )
+            stage_rows(queue, x_stage, xt_scales, h)
+        for h, queue in enumerate((nc.sync, nc.scalar)):
+            stage_rows(queue, w_stage, w_scales, h)
         nc.sync.dma_start(x_win[:].bitcast(I32), xt_words[0].bitcast(I32))
-        nc.scalar.dma_start(w_raw[:], w_words[0].rearrange("p n t -> p (n t)").bitcast(I32))
+        load_words(nc.scalar, w_raw, w_words)
         nc.sync.dma_start(l_pw[:], offs2)
 
-        xs_win = sb_tile([P, T], U8, "xs_win", "slot_xswin")
-        ws_plane = sb_tile([P, R], U8, "ws_plane", "slot_wsplane")
+        warm = sb_tile([P, 16], F32, "warm")
+        nc.gpsimd.memset(warm[:, 0:8], 0.0)
+        nc.scalar.activation(warm[:, 8:16], warm[:, 0:8], COPY)
+
+        xs_win = sb_tile([P, T], U8, "xs_win")
+        ws_plane = sb_tile([P, R], U8, "ws_plane")
         w2s_plane = sb_tile([P, R], U8, "w2s_plane", "slot_w2splane")
-        vss_win = sb_tile([P, S], U8, "vss_win")
+        vss_win = sb_tile([P, S], U8, "vss_win", "slot_vsswin")
         for plane in (xs_win, ws_plane, w2s_plane, vss_win):
             nc.vector.memset(plane[:].bitcast(I32), 0)
 
-        pw = [None] * PACK
-        pv = [None] * PACK
-        for t in (0, 1, 2):
-            pw[t] = sb_tile([P, C], F32, "pw%d" % t)
-            nc.vector.memset(pw[t][:].bitcast(I32), 0)
+        def cleared_board(name, tag=None):
+            board = sb_tile([P, C], F32, name, tag)
+            (nc.gpsimd if tag else nc.vector).memset(board[:].bitcast(I32), 0)
+            return board
 
-        nc.sync.dma_start(l_pv[:], offs3)
+        pw = [cleared_board("pw0"), cleared_board("pw1")]
+
         w2_raw = sb_tile([P, R], I32, "w2_raw", "slot_w2raw")
-        nc.sync.dma_start(w2_raw[:], w2_words[0].rearrange("p n t -> p (n t)").bitcast(I32))
-        for q in range(4):
-            nc.sync.dma_start(
-                w2s_plane[QUAD * q : QUAD * q + 4, :].bitcast(I32),
-                w2_scales[0, 4 * q : 4 * q + 4, :].bitcast(I32),
-            )
+        load_words(nc.sync, w2_raw, w2_words)
+        load_scale_rows(w2s_plane, w2_scales)
+        nc.sync.dma_start(l_pv[:], offs3)
         nc.sync.dma_start(l_vs[:], offs6)
-        vs_win = sb_tile([P, S], I32, "vs_win")
-        nc.sync.dma_start(vs_win[:], vs_words[0].rearrange("p n t -> p (n t)").bitcast(I32))
-        for q in range(4):
-            nc.sync.dma_start(
-                vss_win[QUAD * q : QUAD * q + 4, :].bitcast(I32),
-                vs_scales[0, 4 * q : 4 * q + 4, :].bitcast(I32),
-            )
+        vs_win = sb_tile([P, S], I32, "vs_win", "slot_vswin")
+        load_words(nc.sync, vs_win, vs_words)
+        load_scale_rows(vss_win, vs_scales)
         nc.sync.dma_start(l_win[:], offs4)
         nc.sync.dma_start(l_los[:], offs5)
         sa_t = sb_tile([P, PACK], F32, "sa_t")
@@ -101,107 +123,105 @@ def tile_picked_tokens_plain_twin_winnersides_store_plain_kernel(
         nc.sync.dma_start(sa_t[:], sa.rearrange("(p t) o -> p (t o)", t=PACK))
         nc.sync.dma_start(sb_t[:], sb.rearrange("(p t) o -> p (t o)", t=PACK))
 
-        ws_i = ws_plane[:].bitcast(I32)
-        for q in range(4):
-            nc.vector.tensor_copy(
-                ws_i[QUAD * q : QUAD * q + 4, :], w_stage[0:4, q * (R // 4) : (q + 1) * (R // 4)]
+        def deal(dst, src, run, t0=0, t1=PACK, move=nc.vector.tensor_copy):
+            move(
+                dst[:].rearrange("p (t m i) -> p m t i", t=t1 - t0, i=run),
+                src[:].rearrange("p (m i t) -> p m t i", t=PACK, i=run)[:, :, t0:t1, :],
             )
 
-        xs_i = xs_win[:].bitcast(I32)
-        for q in range(4):
-            h, k = divmod(q, 2)
-            nc.vector.tensor_copy(
-                xs_i[QUAD * q : QUAD * q + 4, :],
-                x_stage[64 * h : 64 * h + 4, k * (T // 4) : (k + 1) * (T // 4)],
-            )
-        xg = sb_tile([P, 2 * J], U8, "xg")
-        xsg = sb_tile([P, J], U8, "xsg")
+        def gather_words(dst, a, b):
+            nc.vector.tensor_copy(dst.bitcast(U16), x_win[:].bitcast(U16).indirect(l_tok[:, cols16(a, b)]))
 
-        def gather_x(a, b):
-            nc.vector.tensor_copy(
-                xg[:].bitcast(U16)[:, a:b], x_win[:].bitcast(U16).indirect(l_tok[:, cols16(a, b)])
-            )
-            nc.vector.tensor_copy(xsg[:, a:b], xs_win[:].indirect(l_tok[:, cols16(a, b)]))
+        def gather_scales(dst, a, b):
+            nc.vector.tensor_copy(dst, xs_win[:].indirect(l_tok[:, cols16(a, b)]))
 
-        wd = sb_tile([P, R], I32, "wd")
-        wsd = sb_tile([P, R], U8, "wsd")
+        CUTS = ((0, 128), (128, 256), (256, 512))
+        spread_rows(xs_win, x_stage)
+        spread_rows(ws_plane, w_stage, True)
+        wd_lo = sb_tile([P, 2 * P], U32, "wd_lo")
+        wd_hi = sb_tile([P, 2 * P], I32, "wd_hi", "slot_wd")
+        wsd_lo = sb_tile([P, 2 * P], U8, "wsd_lo")
+        deal(wsd_lo, ws_plane, 16, 0, 2)
+        xg0 = sb_tile([P, 256], U8, "xg0")
+        xsg0 = sb_tile([P, 128], U8, "xsg0")
+        gather_scales(xsg0[:], 0, 128)
+        gather_words(xg0[:], 0, 128)
+        deal(wd_lo, w_raw[:].bitcast(U32), 4, 0, 2, nc.scalar.copy)
+        deal(wd_hi, w_raw, 4, 2, 4)
+        xg1 = placed([P, 256], U8, "xg1", 0)
+        xsg1 = placed([P, 128], U8, "xsg1", 256)
+        xg2 = placed([P, 512], U8, "xg2", 512)
+        xsg2 = placed([P, 256], U8, "xsg2", 1024)
+        xg = (xg0, xg1, xg2)
+        xsg = (xsg0, xsg1, xsg2)
 
-        def deal(words, plane, raw_words, raw_plane, t0, t1):
-            cols = slice(t0 * P, t1 * P)
-            nc.vector.tensor_copy(
-                words[:, cols].rearrange("p (t m) -> p t m", m=P),
-                raw_words[:].rearrange("p (m t) -> p t m", t=PACK)[:, t0:t1, :],
-            )
-            nc.vector.tensor_copy(
-                plane[:, cols].rearrange("p (t m) -> p t m", m=P),
-                raw_plane[:].rearrange("p (m t) -> p t m", t=PACK)[:, t0:t1, :],
-            )
-
-        def product(bank, words, plane, t, a, b):
+        def product(dst, words, plane, c):
             nc.tensor.matmul_mx(
-                out=bank[:, a:b],
-                lhsT=words[:, t * P : (t + 1) * P].bitcast(FP8X4),
-                lhsT_scale=plane[:, t * P : (t + 1) * P],
-                rhs=xg[:, 2 * a : 2 * b].bitcast(FP4X4),
-                rhs_scale=xsg[:, a:b],
+                out=dst,
+                lhsT=words.bitcast(FP8X4),
+                lhsT_scale=plane,
+                rhs=xg[c][:].bitcast(FP4X4),
+                rhs_scale=xsg[c][:],
                 start=True,
                 stop=True,
             )
 
-        a_ps = [psum.tile([P, J], F32, name="a_ps%d" % t, tag="bank_a%d" % t) for t in range(PACK)]
-        a_sb = [sb_tile([P, J], F32, "a_sb%d" % t) for t in range(PACK)]
-
         def scatter(board, vals, lst, a, b):
-            nc.scalar.activation(board[:].indirect(lst[:, cols16(a, b)]), vals[:, a:b], COPY)
+            nc.scalar.activation(board[:].indirect(lst[:, cols16(a, b)]), vals, COPY)
 
-        def a_piece(t, cuts, on_scalar=False):
-            for a, b in zip(cuts, cuts[1:]):
-                product(a_ps[t], wd, wsd, t, a, b)
-            a, b = cuts[0], cuts[-1]
-            if on_scalar:
-                nc.scalar.activation(a_sb[t][:, a:b], a_ps[t][:, a:b], COPY)
-            else:
-                nc.vector.tensor_copy(a_sb[t][:, a:b], a_ps[t][:, a:b])
-            scatter(pw[t], a_sb[t], l_pw, a, b)
+        first = sb_tile([P, 2, 128], F32, "a_sb0")
+        for t in range(2):
+            bank = psum.tile([P, 128], F32, name="a_ps0%d" % t, tag="bank%d" % t)
+            product(bank[:], wd_lo[:, t * P : (t + 1) * P], wsd_lo[:, t * P : (t + 1) * P], 0)
+            nc.scalar.activation(first[:, t, :], bank[:], COPY)
+        for t in range(2):
+            scatter(pw[t], first[:, t, :], l_pw, 0, 128)
+        for c in (1, 2):
+            a, b = CUTS[c]
+            gather_scales(xsg[c][:], a, b)
+            gather_words(xg[c][:], a, b)
+            bank = psum.tile([P, 2, b - a], F32, name="a_ps%d" % c, tag="bank%d" % (1 + c))
+            for t in range(2):
+                product(bank[:, t, :], wd_lo[:, t * P : (t + 1) * P], wsd_lo[:, t * P : (t + 1) * P], c)
+            vals = sb_tile([P, 2, b - a], F32, "a_sb%d" % c, "slot_piece%d" % c)
+            nc.vector.tensor_copy(vals[:], bank[:])
+            for t in range(2):
+                scatter(pw[t], vals[:, t, :], l_pw, a, b)
+        wsd_hi = placed([P, 2 * P], U8, "wsd_hi", 1280)
+        deal(wsd_hi, ws_plane, 16, 2, 4)
 
-        deal(wd, wsd, w_raw, ws_plane, 0, 1)
-        gather_x(0, 128)
-        a_piece(0, (0, 128), True)
-        deal(wd, wsd, w_raw, ws_plane, 1, 2)
-        a_piece(1, (0, 128))
-        gather_x(128, 256)
-        a_piece(0, (128, 256))
-        a_piece(1, (128, 256))
-        gather_x(256, 512)
-        a_piece(0, (256, 512))
-        a_piece(1, (256, 512))
-        deal(wd, wsd, w_raw, ws_plane, 2, 4)
-        a_piece(2, (0, 512))
-        pw[3] = sb_tile([P, C], F32, "pw3", "slot_xwin")
-        nc.vector.memset(pw[3][:].bitcast(I32), 0)
-        a_piece(3, (0, 512))
+        def whole_row(words, plane, name, bank_tag, tag=None):
+            bank = psum.tile([P, J], F32, name=name + "_ps", tag=bank_tag)
+            for c, (a, b) in enumerate(CUTS):
+                product(bank[:, a:b], words, plane, c)
+            vals = sb_tile([P, J], F32, name, tag)
+            nc.vector.tensor_copy(vals[:], bank[:])
+            return vals
 
-        w2d = sb_tile([P, R], I32, "w2d")
-        w2sd = sb_tile([P, R], U8, "w2sd")
-        deal(w2d, w2sd, w2_raw, w2s_plane, 0, 4)
-        b_ps = [psum.tile([P, J], F32, name="b_ps%d" % t, tag="bank_b%d" % t) for t in range(PACK)]
-        b_sb = [sb_tile([P, J], F32, "b_sb%d" % t, "slot_b%d" % t) for t in range(PACK)]
-        pv_tags = ("slot_wraw", "slot_wsplane", "slot_w2raw", "slot_w2splane")
-        for t in range(PACK):
-            product(b_ps[t], w2d, w2sd, t, 0, J)
-            nc.vector.tensor_copy(b_sb[t][:], b_ps[t][:])
-            pv[t] = sb_tile([P, C], F32, "pv%d" % t, pv_tags[t])
-            nc.vector.memset(pv[t][:].bitcast(I32), 0)
+        for t in (2, 3):
+            vals = whole_row(wd_hi[:, (t - 2) * P : (t - 1) * P], wsd_hi[:, (t - 2) * P : (t - 1) * P], "a_row%d" % t, "bank3", "slot_a%d" % t)
+            pw.append(cleared_board("pw%d" % t, "slot_piece%d" % (t - 1)))
+            scatter(pw[t], vals[:], l_pw, 0, J)
 
-        vg = sb_tile([P, N], U32, "vg")
-        vsg = sb_tile([P, N], U8, "vsg")
+        w2d = sb_tile([P, R], I32, "w2d", "slot_wd")
+        w2sd = placed([P, R], U8, "w2sd", 1280)
+        deal(w2d, w2_raw, 4)
+        deal(w2sd, w2s_plane, 16)
+        b_sb = [
+            whole_row(w2d[:, t * P : (t + 1) * P], w2sd[:, t * P : (t + 1) * P], "b_row%d" % t, "bank%d" % (4 + t), "slot_b%d" % t)
+            for t in range(PACK)
+        ]
+        vg = sb_tile([P, N], U32, "vg", "slot_w2raw")
+        vsg = sb_tile([P, N], U8, "vsg", "slot_w2splane")
         nc.vector.tensor_copy(vg[:], vs_win[:].bitcast(U32).indirect(l_vs[:]))
         nc.vector.tensor_copy(vsg[:], vss_win[:].indirect(l_vs[:]))
+        pv = []
 
         ph = [None] * PACK
         pl = [None] * PACK
         for t in range(PACK):
-            scatter(pv[t], b_sb[t], l_pv, 0, J)
+            pv.append(cleared_board("pv%d" % t, ("slot_a2", "slot_a3", "slot_b0", "slot_b1")[t]))
+            scatter(pv[t], b_sb[t][:], l_pv, 0, J)
             ph[t] = sb_tile([P, C], F32, "ph%d" % t, "slot_ph%d" % t)
             pl[t] = sb_tile([P, C], F32, "pl%d" % t, "slot_pl%d" % t)
             nc.vector.tensor_tensor(ph[t][:], pw[t][:], pv[t][:], ALU.max)
@@ -248,20 +268,26 @@ def tile_picked_tokens_plain_twin_winnersides_store_plain_kernel(
 
         win_planes = fetch(0, ph, l_win, sa_t, "slot_b3")
         win_q = quantise(weave(win_planes, 0, O, "w"), "w")
-        win_ps = [last_product(*win_q, half, "bank_a%d" % half) for half in range(2)]
+        win_ps = [last_product(*win_q, half, "bank%d" % half) for half in range(2)]
         los_planes = fetch(1, pl, l_los, sb_t, "slot_ph3")
         y_win = sb_tile([P, 2, O], F32, "y_win", "slot_pl3")
         for half in range(2):
             nc.scalar.copy(y_win[:, half, :], win_ps[half][:])
         nc.sync.dma_start(out.rearrange("(h p) d -> p h d", h=2)[:, :, 0:O], y_win[:])
         HALF = U // 2
-        los_w = [weave(los_planes, j * HALF, (j + 1) * HALF, "l%d" % j) for j in range(2)]
+        los_w = [sb_tile([P, HALF, PACK], BF16, "woven_l%d" % j) for j in range(2)]
+        for t0, t1 in ((0, PACK - 1), (PACK - 1, PACK)):
+            for j in range(2):
+                nc.vector.tensor_copy(
+                    los_w[j][:, :, t0:t1].rearrange("p (c i) t -> p c t i", i=4),
+                    los_planes[:, t0:t1, j * HALF : (j + 1) * HALF].rearrange("p t (c i) -> p c t i", i=4),
+                )
         los_q = [quantise(los_w[j], "l%d" % j) for j in range(2)]
         for j in range(2):
             cols = slice(O + j * HALF, O + (j + 1) * HALF)
             for half in range(2):
                 rows = slice(half * P, (half + 1) * P)
-                y_ps = last_product(*los_q[j], half, "bank_b%d" % (2 * j + half))
+                y_ps = last_product(*los_q[j], half, "bank%d" % (4 + 2 * j + half))
                 y_sb = sb_tile([P, HALF], F32, "y_los%d%d" % (j, half))
                 if half == 0:
                     nc.scalar.copy(y_sb[:], y_ps[:])

@@ -90,10 +90,6 @@ def tile_picked_tokens_plain_twin_winnersides_store_plain_kernel(
         load_words(nc.scalar, w_raw, w_words)
         nc.sync.dma_start(l_pw[:], offs2)
 
-        warm = sb_tile([P, 16], F32, "warm")
-        nc.gpsimd.memset(warm[:, 0:8], 0.0)
-        nc.scalar.activation(warm[:, 8:16], warm[:, 0:8], COPY)
-
         xs_win = sb_tile([P, T], U8, "xs_win")
         ws_plane = sb_tile([P, R], U8, "ws_plane")
         w2s_plane = sb_tile([P, R], U8, "w2s_plane", "slot_w2splane")

from contextlib import ExitStack

import concourse.mybir as mybir

K, J, R, T, C, O, U, D, N, S = 512, 512, 512, 1024, 1024, 256, 256, 512, 256, 1024
FLOPS = 2 * (2 * K * R * J + R * N * D)

F32 = mybir.dt.float32
BF16 = mybir.dt.bfloat16
I32 = mybir.dt.int32
U32 = mybir.dt.uint32
U16 = mybir.dt.uint16
U8 = mybir.dt.uint8
FP8X4 = mybir.dt.float8_e4m3fn_x4
FP4X4 = mybir.dt.float4_e2m1fn_x4
COPY = mybir.ActivationFunctionType.Copy
ALU = mybir.AluOpType

P = 128
PACK = 4
QUAD = 32


def tile_picked_tokens_plain_twin_winnersides_store_plain_kernel(
    tc, xt_words, xt_scales, w_words, w_scales, w2_words, w2_scales, sa, sb, vs_words, vs_scales,
    offs, offs2, offs3, offs4, offs5, offs6, out
):
    nc = tc.nc
    with ExitStack() as ctx:
        lists = ctx.enter_context(tc.tile_pool(name="lists", bufs=1))
        pool = ctx.enter_context(tc.tile_pool(name="pool", bufs=1))
        reuse = ctx.enter_context(tc.tile_pool(name="reuse", bufs=1))
        psum = ctx.enter_context(tc.psum_pool(name="psum", bufs=1))

        def sb_tile(shape, dtype, name, tag=None):
            return pool.tile(shape, dtype, name=name, tag=tag or name, align_bytes=64)

        def placed(shape, dtype, name, offset):
            return reuse.tile(shape, dtype, name=name, offset=offset, align_bytes=64)

        def list_tile(src, name):
            return lists.tile([P, src.shape[1]], U16, name=name)

        l_tok = list_tile(offs, "l_tok")
        l_pw = list_tile(offs2, "l_pw")
        l_pv = list_tile(offs3, "l_pv")
        l_win = list_tile(offs4, "l_win")
        l_los = list_tile(offs5, "l_los")
        l_vs = list_tile(offs6, "l_vs")

        def cols16(a, b):
            return slice(a // 16, b // 16)

        x_stage = sb_tile([P, 2 * T // 4], I32, "x_stage")
        w_stage = sb_tile([P, 2 * R // 4], I32, "w_stage")
        x_win = sb_tile([P, 2 * T], U8, "x_win")
        w_raw = placed([P, R], I32, "w_raw", 0)

        def stage_rows(queue, stage, src, h):
            rows = src[0].bitcast(I32).rearrange("(h q i) c -> h i q c", h=2, q=2)
            queue.dma_start(stage[64 * h : 64 * h + 4, :].rearrange("i (q c) -> i q c", q=2), rows[h])

        def spread_rows(plane, stage, share=False):
            words = plane[:].bitcast(I32)
            width = words.shape[1]
            for q in range(4):
                h, k = divmod(q, 2)
                dst = words[QUAD * q : QUAD * q + 4, :]
                src = stage[64 * h : 64 * h + 4, k * width : (k + 1) * width]
                if share and k == 0:
                    nc.scalar.copy(dst.bitcast(U32), src.bitcast(U32))
                else:
                    nc.vector.tensor_copy(dst, src)

        def load_scale_rows(plane, src):
            for q in range(4):
                nc.sync.dma_start(
                    plane[QUAD * q : QUAD * q + 4, :].bitcast(I32), src[0, 4 * q : 4 * q + 4, :].bitcast(I32)
                )

        def load_words(queue, dst, src):
            queue.dma_start(dst[:], src[0].rearrange("p n t -> p (n t)").bitcast(I32))

        nc.sync.dma_start(l_tok[:], offs)
        for h, queue in enumerate((nc.sync, nc.scalar)):
            stage_rows(queue, x_stage, xt_scales, h)
        for h, queue in enumerate((nc.sync, nc.scalar)):
            stage_rows(queue, w_stage, w_scales, h)
        nc.sync.dma_start(x_win[:].bitcast(I32), xt_words[0].bitcast(I32))
        load_words(nc.scalar, w_raw, w_words)
        nc.sync.dma_start(l_pw[:], offs2)

        xs_win = sb_tile([P, T], U8, "xs_win")
        ws_plane = sb_tile([P, R], U8, "ws_plane")
        w2s_plane = sb_tile([P, R], U8, "w2s_plane", "slot_w2splane")
        vss_win = sb_tile([P, S], U8, "vss_win", "slot_vsswin")
        for plane in (xs_win, ws_plane, w2s_plane, vss_win):
            nc.vector.memset(plane[:].bitcast(I32), 0)

        def cleared_board(name, tag=None):
            board = sb_tile([P, C], F32, name, tag)
            (nc.gpsimd if tag else nc.vector).memset(board[:].bitcast(I32), 0)
            return board

        pw = [cleared_board("pw0"), cleared_board("pw1")]

        w2_raw = sb_tile([P, R], I32, "w2_raw", "slot_w2raw")
        load_words(nc.sync, w2_raw, w2_words)
        load_scale_rows(w2s_plane, w2_scales)
        nc.sync.dma_start(l_pv[:], offs3)
        nc.sync.dma_start(l_vs[:], offs6)
        vs_win = sb_tile([P, S], I32, "vs_win", "slot_vswin")
        load_words(nc.sync, vs_win, vs_words)
        load_scale_rows(vss_win, vs_scales)
        nc.sync.dma_start(l_win[:], offs4)
        nc.sync.dma_start(l_los[:], offs5)
        sa_t = sb_tile([P, PACK], F32, "sa_t")
        sb_t = sb_tile([P, PACK], F32, "sb_t")
        nc.sync.dma_start(sa_t[:], sa.rearrange("(p t) o -> p (t o)", t=PACK))
        nc.sync.dma_start(sb_t[:], sb.rearrange("(p t) o -> p (t o)", t=PACK))

        def deal(dst, src, run, t0=0, t1=PACK, move=nc.vector.tensor_copy):
            move(
                dst[:].rearrange("p (t m i) -> p m t i", t=t1 - t0, i=run),
                src[:].rearrange("p (m i t) -> p m t i", t=PACK, i=run)[:, :, t0:t1, :],
            )

        def gather_words(dst, a, b):
            nc.vector.tensor_copy(dst.bitcast(U16), x_win[:].bitcast(U16).indirect(l_tok[:, cols16(a, b)]))

        def gather_scales(dst, a, b):
            nc.vector.tensor_copy(dst, xs_win[:].indirect(l_tok[:, cols16(a, b)]))

        CUTS = ((0, 128), (128, 256), (256, 512))
        spread_rows(xs_win, x_stage)
        spread_rows(ws_plane, w_stage, True)
        wd_lo = sb_tile([P, 2 * P], U32, "wd_lo")
        wd_hi = sb_tile([P, 2 * P], I32, "wd_hi", "slot_wd")
        wsd_lo = sb_tile([P, 2 * P], U8, "wsd_lo")
        deal(wsd_lo, ws_plane, 16, 0, 2)
        xg0 = sb_tile([P, 256], U8, "xg0")
        xsg0 = sb_tile([P, 128], U8, "xsg0")
        gather_scales(xsg0[:], 0, 128)
        gather_words(xg0[:], 0, 128)
        deal(wd_lo, w_raw[:].bitcast(U32), 4, 0, 2, nc.scalar.copy)
        deal(wd_hi, w_raw, 4, 2, 4)
        xg1 = placed([P, 256], U8, "xg1", 0)
        xsg1 = placed([P, 128], U8, "xsg1", 256)
        xg2 = placed([P, 512], U8, "xg2", 512)
        xsg2 = placed([P, 256], U8, "xsg2", 1024)
        xg = (xg0, xg1, xg2)
        xsg = (xsg0, xsg1, xsg2)

        def product(dst, words, plane, c):
            nc.tensor.matmul_mx(
                out=dst,
                lhsT=words.bitcast(FP8X4),
                lhsT_scale=plane,
                rhs=xg[c][:].bitcast(FP4X4),
                rhs_scale=xsg[c][:],
                start=True,
                stop=True,
            )

        def scatter(board, vals, lst, a, b):
            nc.scalar.activation(board[:].indirect(lst[:, cols16(a, b)]), vals, COPY)

        first = sb_tile([P, 2, 128], F32, "a_sb0")
        for t in range(2):
            bank = psum.tile([P, 128], F32, name="a_ps0%d" % t, tag="bank%d" % t)
            product(bank[:], wd_lo[:, t * P : (t + 1) * P], wsd_lo[:, t * P : (t + 1) * P], 0)
            nc.scalar.activation(first[:, t, :], bank[:], COPY)
        for t in range(2):
            scatter(pw[t], first[:, t, :], l_pw, 0, 128)
        for c in (1, 2):
            a, b = CUTS[c]
            gather_scales(xsg[c][:], a, b)
            gather_words(xg[c][:], a, b)
            bank = psum.tile([P, 2, b - a], F32, name="a_ps%d" % c, tag="bank%d" % (1 + c))
            for t in range(2):
                product(bank[:, t, :], wd_lo[:, t * P : (t + 1) * P], wsd_lo[:, t * P : (t + 1) * P], c)
            vals = sb_tile([P, 2, b - a], F32, "a_sb%d" % c, "slot_piece%d" % c)
            nc.vector.tensor_copy(vals[:], bank[:])
            for t in range(2):
                scatter(pw[t], vals[:, t, :], l_pw, a, b)
        wsd_hi = placed([P, 2 * P], U8, "wsd_hi", 1280)
        deal(wsd_hi, ws_plane, 16, 2, 4)

        def whole_row(words, plane, name, bank_tag, tag=None):
            bank = psum.tile([P, J], F32, name=name + "_ps", tag=bank_tag)
            for c, (a, b) in enumerate(CUTS):
                product(bank[:, a:b], words, plane, c)
            vals = sb_tile([P, J], F32, name, tag)
            nc.vector.tensor_copy(vals[:], bank[:])
            return vals

        for t in (2, 3):
            vals = whole_row(wd_hi[:, (t - 2) * P : (t - 1) * P], wsd_hi[:, (t - 2) * P : (t - 1) * P], "a_row%d" % t, "bank3", "slot_a%d" % t)
            pw.append(cleared_board("pw%d" % t, "slot_piece%d" % (t - 1)))
            scatter(pw[t], vals[:], l_pw, 0, J)

        w2d = sb_tile([P, R], I32, "w2d", "slot_wd")
        w2sd = placed([P, R], U8, "w2sd", 1280)
        deal(w2d, w2_raw, 4)
        deal(w2sd, w2s_plane, 16)
        b_sb = [
            whole_row(w2d[:, t * P : (t + 1) * P], w2sd[:, t * P : (t + 1) * P], "b_row%d" % t, "bank%d" % (4 + t), "slot_b%d" % t)
            for t in range(PACK)
        ]
        vg = sb_tile([P, N], U32, "vg", "slot_w2raw")
        vsg = sb_tile([P, N], U8, "vsg", "slot_w2splane")
        nc.vector.tensor_copy(vg[:], vs_win[:].bitcast(U32).indirect(l_vs[:]))
        nc.vector.tensor_copy(vsg[:], vss_win[:].indirect(l_vs[:]))
        pv = []

        ph = [None] * PACK
        pl = [None] * PACK
        for t in range(PACK):
            pv.append(cleared_board("pv%d" % t, ("slot_a2", "slot_a3", "slot_b0", "slot_b1")[t]))
            scatter(pv[t], b_sb[t][:], l_pv, 0, J)
            ph[t] = sb_tile([P, C], F32, "ph%d" % t, "slot_ph%d" % t)
            pl[t] = sb_tile([P, C], F32, "pl%d" % t, "slot_pl%d" % t)
            nc.vector.tensor_tensor(ph[t][:], pw[t][:], pv[t][:], ALU.max)
            nc.vector.tensor_tensor(pl[t][:], pw[t][:], pv[t][:], ALU.min)

        def fetch(side, boards, lst, gain, tag):
            planes = sb_tile([P, PACK, O], BF16, "planes%d" % side, tag)
            for t in range(PACK):
                nc.scalar.activation(
                    planes[:, t, :], boards[t][:].indirect(lst[:]), COPY, scale=gain[:, t : t + 1]
                )
            return planes

        def weave(planes, a, b, name):
            woven = sb_tile([P, b - a, PACK], BF16, "woven" + name)
            nc.vector.tensor_copy(
                woven[:].rearrange("p (c i) t -> p c t i", i=4),
                planes[:, :, a:b].rearrange("p t (c i) -> p c t i", i=4),
            )
            return woven

        def quantise(woven, name):
            width = woven.shape[1]
            hq = sb_tile([P, width], U32, "hq" + name)
            hs = sb_tile([P, width], U8, "hs" + name)
            nc.vector.quantize_mx(
                out=hq[:].bitcast(FP8X4), scales=hs[:], in_=woven[:].rearrange("p c t -> p (c t)")
            )
            return hq, hs

        def last_product(hq, hs, half, bank):
            rows = slice(half * P, (half + 1) * P)
            y_ps = psum.tile([P, hq.shape[1]], F32, name="y_" + bank, tag=bank)
            nc.tensor.matmul_mx(
                out=y_ps[:],
                lhsT=vg[:, rows].bitcast(FP8X4),
                lhsT_scale=vsg[:, rows],
                rhs=hq[:].bitcast(FP8X4),
                rhs_scale=hs[:],
                start=True,
                stop=True,
            )
            return y_ps

        win_planes = fetch(0, ph, l_win, sa_t, "slot_b3")
        win_q = quantise(weave(win_planes, 0, O, "w"), "w")
        win_ps = [last_product(*win_q, half, "bank%d" % half) for half in range(2)]
        los_planes = fetch(1, pl, l_los, sb_t, "slot_ph3")
        y_win = sb_tile([P, 2, O], F32, "y_win", "slot_pl3")
        for half in range(2):
            nc.scalar.copy(y_win[:, half, :], win_ps[half][:])
        nc.sync.dma_start(out.rearrange("(h p) d -> p h d", h=2)[:, :, 0:O], y_win[:])
        HALF = U // 2
        los_w = [sb_tile([P, HALF, PACK], BF16, "woven_l%d" % j) for j in range(2)]
        for t0, t1 in ((0, PACK - 1), (PACK - 1, PACK)):
            for j in range(2):
                nc.vector.tensor_copy(
                    los_w[j][:, :, t0:t1].rearrange("p (c i) t -> p c t i", i=4),
                    los_planes[:, t0:t1, j * HALF : (j + 1) * HALF].rearrange("p t (c i) -> p c t i", i=4),
                )
        los_q = [quantise(los_w[j], "l%d" % j) for j in range(2)]
        for j in range(2):
            cols = slice(O + j * HALF, O + (j + 1) * HALF)
            for half in range(2):
                rows = slice(half * P, (half + 1) * P)
                y_ps = last_product(*los_q[j], half, "bank%d" % (4 + 2 * j + half))
                y_sb = sb_tile([P, HALF], F32, "y_los%d%d" % (j, half))
                if half == 0:
                    nc.scalar.copy(y_sb[:], y_ps[:])
                    nc.scalar.dma_start(out[rows, cols], y_sb[:])
                else:
                    nc.vector.tensor_copy(y_sb[:], y_ps[:])
                    nc.sync.dma_start(out[rows, cols], y_sb[:])
